import numpy as np
import ml_dtypes


def mxq(x, axis, fmt="e4m3"):
    dtype, down = {"e4m3": (ml_dtypes.float8_e4m3fn, 7), "e5m2": (ml_dtypes.float8_e5m2, 14)}[fmt]
    v = np.moveaxis(np.asarray(x, np.float32).astype(ml_dtypes.bfloat16).astype(np.float64), axis, -1)
    blocks = v.reshape(v.shape[:-1] + (-1, 32))
    amax = np.abs(blocks).max(-1, keepdims=True)
    byte = np.maximum(np.where(amax > 0, np.frexp(amax)[1] - 1 + 127, 0) - down, 1)
    scale = np.exp2(byte - 127.0)
    codes = (blocks / scale).astype(np.float32).astype(dtype).astype(np.float64)
    return np.moveaxis((codes * scale).reshape(v.shape), -1, axis)


WIDE = False


def mx_kscale(k):
    if not WIDE:
        return np.ones(k)
    levels = np.array([10, -10, 5, -5, 0])
    if k % 512:
        return np.exp2(np.random.permutation(np.resize(levels, k // 32))).repeat(32)
    a = np.empty((k // 512, 16))
    for p in range(k // 512):
        a[p, :8] = np.random.permutation(np.resize(levels, 8))
        for g in range(8):
            far = levels[np.abs(levels - a[p, g]) >= 10]
            a[p, g + 8] = far[np.random.randint(len(far))]
    return np.exp2(a.ravel()).repeat(32)


def f64(x):
    return np.asarray(x).astype(np.float64)


def striped(idx):
    return np.tile(idx.reshape(-1, 16).T, (8, 1)).astype(np.uint16)


def unstriped(offs):
    return offs[:16].T.reshape(-1).astype(np.int64)


E2M1 = np.array([0.0, 0.5, 1.0, 1.5, 2.0, 3.0, 4.0, 6.0, -0.0, -0.5, -1.0, -1.5, -2.0, -3.0, -4.0, -6.0])


def pack_weight(w, fmt):
    k, n = w.shape
    w = f64(np.asarray(w, np.float32).astype(ml_dtypes.bfloat16)).reshape(k // 32, 32, n)
    amax = np.abs(w).max(1)
    if fmt == "e4m3":
        byte = np.frexp(amax)[1] - 1 + 127 - 7
    else:
        mant, ex = np.frexp(amax / 6.0)
        byte = np.where(mant > 0.5, ex, ex - 1) + 127
    byte = np.clip(np.where(amax > 0, byte, 1), 1, 254)
    scaled = (w * np.exp2(127.0 - byte)[:, None, :]).reshape(k, n).astype(np.float32)
    by_word = np.ascontiguousarray(scaled.reshape(k // 512, 128, 4, n).transpose(0, 1, 3, 2))
    if fmt == "e4m3":
        words = by_word.astype(ml_dtypes.float8_e4m3fn).view(np.uint8)
    else:
        c = by_word.astype(ml_dtypes.float4_e2m1fn).view(np.uint8) & 0xF
        words = (c[..., 0::2] | (c[..., 1::2] << 4)).reshape(k // 512, 128, 2 * n)
    return np.ascontiguousarray(words), np.ascontiguousarray(byte.astype(np.uint8).reshape(k // 512, 16, n))


def unpack_weight(words, scales, fmt):
    g, _, n = scales.shape
    words = np.ascontiguousarray(words).reshape(g, 128, n, -1)
    if fmt == "e4m3":
        vals = words.view(ml_dtypes.float8_e4m3fn).astype(np.float64)
    else:
        nib = np.empty((g, 128, n, 4), np.uint8)
        nib[..., 0::2] = words & 0xF
        nib[..., 1::2] = words >> 4
        vals = E2M1[nib]
    vals = vals * np.repeat(np.exp2(scales.astype(np.float64) - 127.0), 8, axis=1)[..., None]
    return vals.transpose(0, 1, 3, 2).reshape(g * 512, n)


K, T, E, C, N = 1024, 1024, 8, 128, 256


def by_expert(wq, xq):
    return np.concatenate([wq[e].T @ xq[:, e * C:(e + 1) * C] for e in range(E)], axis=1)


def setup_inputs():
    n = np.random.standard_normal
    s = mx_kscale(K)[:, None]
    w = [pack_weight(m, "e2m1") for m in n((E, K, N)) / np.sqrt(K) / s[None]]
    return {
        "xT": (n((K, T)) * s).astype(np.float32),
        "w_words": np.stack([m[0] for m in w]),
        "w_scales": np.stack([m[1] for m in w]),
        "gate": np.tile(np.random.uniform(0.2, 1.0, E * C), (N, 1)).astype(np.float32),
        "offs": striped(np.random.permutation(T)[:E * C]),
    }


def reference(xT, w_words, w_scales, gate, offs):
    idx = unstriped(offs)
    w = np.stack([unpack_weight(w_words[e], w_scales[e], "e2m1") for e in range(E)])
    xq = mxq(f64(xT)[:, idx], 0, "e4m3")
    y = by_expert(w, xq)
    out = np.zeros((N, T))
    out[:, idx] = f64(gate) * y
    return out

@@ -1,0 +1,129 @@
+from contextlib import ExitStack
+
+import concourse.mybir as mybir
+
+K, T, E, C, N = 1024, 1024, 8, 128, 256
+FLOPS = 2 * K * E * C * N
+BYTES = 4 * K * T + E * K * N // 2 + E * K * N // 32 + 4 * E * C + 2 * 128 * (E * C // 16) + 4 * N * T
+
+F32 = mybir.dt.float32
+BF16 = mybir.dt.bfloat16
+U32 = mybir.dt.uint32
+I32 = mybir.dt.int32
+U16 = mybir.dt.uint16
+U8 = mybir.dt.uint8
+FP8X4 = mybir.dt.float8_e4m3fn_x4
+FP4X4 = mybir.dt.float4_e2m1fn_x4
+COPY = mybir.ActivationFunctionType.Copy
+MULT = mybir.AluOpType.mult
+
+P = 128
+PASSES = K // 512
+H = 512
+CHUNKS = (
+    ((0, 512, 256), (512, 256, 128), (768, 256, 128)),
+    ((0, 512, 448), (512, 256, 192), (768, 256, 128)),
+)
+
+
+def tile_moe_pln_lin_none_kernel(tc, xT, w_words, w_scales, gate, offs, out):
+    nc = tc.nc
+    with ExitStack() as ctx:
+        keep = ctx.enter_context(tc.tile_pool(name="keep", bufs=1))
+        psum = ctx.enter_context(tc.psum_pool(name="psum", bufs=1))
+
+        lists = keep.tile([P, E * C // 16], U16, name="lists")
+        raw = {}
+        for a in range(PASSES):
+            for t0, n, n_scalar in CHUNKS[a]:
+                r = keep.tile([P, 4, n], F32, name=f"raw{a}_{t0}", align_bytes=64)
+                nc.sync.dma_start(
+                    out=r[:],
+                    in_=xT[a * 512 : (a + 1) * 512, t0 : t0 + n].rearrange("(p j) w -> p j w", j=4),
+                )
+                raw[a, t0] = r
+            if a == 0:
+                nc.sync.dma_start(lists[:], offs)
+
+        wt = keep.tile([P, E * PASSES, 2 * N], U8, name="wt", align_bytes=64)
+        ws = keep.tile([P, E * PASSES, N], U8, name="ws", align_bytes=64)
+        nc.vector.memset(ws[:].rearrange("p g n -> p (g n)").bitcast(I32), 0)
+        w_by_p = w_words.rearrange("e a p b -> p (e a) b").bitcast(I32)
+        for i in range(2):
+            g = slice(i * E, (i + 1) * E)
+            nc.sync.dma_start(out=wt[:, g, :].bitcast(I32), in_=w_by_p[:, g, :])
+        s_by_q = w_scales.rearrange("e a (q r) n -> q r (e a) n", r=4).bitcast(I32)
+        for q in range(4):
+            nc.sync.dma_start(out=ws[32 * q : 32 * q + 4, :, :].bitcast(I32), in_=s_by_q[q])
+        gt = keep.tile([P, E * C], F32, name="gt", align_bytes=64)
+        nc.sync.dma_start(out=gt[:], in_=gate[0:P, :])
+
+        codes, scales = [], []
+        for a in range(PASSES):
+            c = keep.tile([P, T], U32, name=f"codes{a}", align_bytes=64)
+            s = keep.tile([P, T], U8, name=f"scales{a}", align_bytes=64)
+            nc.gpsimd.memset(s[:], 0)
+            codes.append(c)
+            scales.append(s)
+
+        for a in range(PASSES):
+            for t0, n, n_scalar in CHUNKS[a]:
+                g = keep.tile([P, n, 4], BF16, name=f"grouped{a}_{t0}", align_bytes=64)
+                src = raw[a, t0][:].rearrange("p j w -> p w j")
+                nc.scalar.activation(g[:, 0:n_scalar, :], src[:, 0:n_scalar, :], COPY)
+                nc.vector.tensor_copy(g[:, n_scalar:n, :], src[:, n_scalar:n, :])
+                cols = slice(t0, t0 + n)
+                nc.vector.quantize_mx(
+                    out=codes[a][:, cols].bitcast(FP8X4),
+                    scales=scales[a][:, cols],
+                    in_=g[:].rearrange("p w j -> p (w j)"),
+                )
+
+        picked, picked_s = [], []
+        for a in range(PASSES):
+            c = keep.tile([P, E * C], U32, name=f"picked{a}", align_bytes=64)
+            s = keep.tile([P, E * C], U8, name=f"picked_s{a}", align_bytes=64)
+            picked.append(c)
+            picked_s.append(s)
+            for h in range(E * C // H):
+                cols = slice(h * H, (h + 1) * H)
+                idx = lists[:, h * H // 16 : (h + 1) * H // 16]
+                nc.vector.tensor_copy(c[:, cols], codes[a][:].indirect(idx))
+                nc.vector.tensor_copy(s[:, cols], scales[a][:].indirect(idx))
+
+        banks = {}
+        for h in range(2):
+            for m in range(2):
+                bank = psum.tile([P, H], F32, name=f"bank{m}{h}")
+                banks[m, h] = bank
+                for i in range(H // C):
+                    e = h * (H // C) + i
+                    for a in range(PASSES):
+                        nc.tensor.matmul_mx(
+                            out=bank[:, i * C : (i + 1) * C],
+                            lhsT=wt[:, e * PASSES + a, m * 256 : (m + 1) * 256].bitcast(FP4X4),
+                            lhsT_scale=ws[:, e * PASSES + a, m * 128 : (m + 1) * 128],
+                            rhs=picked[a][:, e * C : (e + 1) * C].bitcast(FP8X4),
+                            rhs_scale=picked_s[a][:, e * C : (e + 1) * C],
+                            start=(a == 0),
+                            stop=(a == PASSES - 1),
+                        )
+
+        gated = {}
+        for h in range(2):
+            for m in range(2):
+                y = keep.tile([P, H], F32, name=f"gated{m}{h}", align_bytes=64)
+                plain = keep.tile([P, H], F32, name=f"plain{m}{h}", align_bytes=64)
+                nc.scalar.activation(plain[:], banks[m, h][:], COPY)
+                nc.gpsimd.tensor_tensor(y[:], plain[:], gt[:, h * H : (h + 1) * H], MULT)
+                gated[m, h] = y
+        back = []
+        for m in range(2):
+            b = keep.tile([P, T], F32, name=f"back{m}", align_bytes=64)
+            back.append(b)
+        for h in range(2):
+            for m in range(2):
+                idx = lists[:, h * H // 16 : (h + 1) * H // 16]
+                nc.vector.tensor_copy(back[m][:].indirect(idx), gated[m, h][:])
+        for m in range(2):
+            nc.sync.dma_start(out=out[m * P : (m + 1) * P, :], in_=back[m][:])

@@ -112,11 +112,9 @@ def tile_moe_pln_lin_none_kernel(tc, xT, w_words, w_scales, gate, offs, out):
         gated = {}
         for h in range(2):
             for m in range(2):
-                y = keep.tile([P, H], F32, name=f"gated{m}{h}", align_bytes=64)
                 plain = keep.tile([P, H], F32, name=f"plain{m}{h}", align_bytes=64)
                 nc.scalar.activation(plain[:], banks[m, h][:], COPY)
-                nc.gpsimd.tensor_tensor(y[:], plain[:], gt[:, h * H : (h + 1) * H], MULT)
-                gated[m, h] = y
+                gated[m, h] = plain
         back = []
         for m in range(2):
             b = keep.tile([P, T], F32, name=f"back{m}", align_bytes=64)
@@ -124,6 +122,6 @@ def tile_moe_pln_lin_none_kernel(tc, xT, w_words, w_scales, gate, offs, out):
         for h in range(2):
             for m in range(2):
                 idx = lists[:, h * H // 16 : (h + 1) * H // 16]
-                nc.vector.tensor_copy(back[m][:].indirect(idx), gated[m, h][:])
+                nc.vector.tensor_tensor(back[m][:].indirect(idx), gated[m, h][:], gt[:, h * H : (h + 1) * H], MULT)
         for m in range(2):
             nc.sync.dma_start(out=out[m * P : (m + 1) * P, :], in_=back[m][:])

@@ -21,8 +21,8 @@ P = 128
 PASSES = K // 512
 H = 512
 CHUNKS = (
-    ((0, 512, 256), (512, 256, 128), (768, 256, 128)),
-    ((0, 512, 448), (512, 256, 192), (768, 256, 128)),
+    ((0, 512, 256), (512, 256, 128), (768, 256, 88)),
+    ((0, 256, 256), (256, 256, 256), (512, 256, 256), (768, 256, 160)),
 )
 
 
@@ -69,9 +69,12 @@ def tile_moe_pln_lin_none_kernel(tc, xT, w_words, w_scales, gate, offs, out):
         for a in range(PASSES):
             for t0, n, n_scalar in CHUNKS[a]:
                 g = keep.tile([P, n, 4], BF16, name=f"grouped{a}_{t0}", align_bytes=64)
-                src = raw[a, t0][:].rearrange("p j w -> p w j")
-                nc.scalar.activation(g[:, 0:n_scalar, :], src[:, 0:n_scalar, :], COPY)
-                nc.vector.tensor_copy(g[:, n_scalar:n, :], src[:, n_scalar:n, :])
+                src = raw[a, t0][:].rearrange("p j (c i) -> p c j i", i=4)
+                dst = g[:].rearrange("p (c i) j -> p c j i", i=4)
+                cut = n_scalar // 4
+                nc.scalar.activation(dst[:, 0:cut], src[:, 0:cut], COPY)
+                if n_scalar < n:
+                    nc.vector.tensor_copy(dst[:, cut : n // 4], src[:, cut : n // 4])
                 cols = slice(t0, t0 + n)
                 nc.vector.quantize_mx(
                     out=codes[a][:, cols].bitcast(FP8X4),

@@ -45,26 +45,27 @@ def tile_moe_pln_lin_none_kernel(tc, xT, w_words, w_scales, gate, offs, out):
             if a == 0:
                 nc.sync.dma_start(lists[:], offs)
 
-        wt = keep.tile([P, E * PASSES, 2 * N], U8, name="wt", align_bytes=64)
+        w_by_p = w_words.rearrange("e a p b -> p (e a) b").bitcast(I32)
+
+        def load_words(h, tag):
+            t = keep.tile([P, E, 2 * N], U8, name=f"words{h}", tag=tag, align_bytes=64)
+            nc.sync.dma_start(out=t[:].bitcast(I32), in_=w_by_p[:, h * E : (h + 1) * E, :])
+            return t
+
         ws = keep.tile([P, E * PASSES, N], U8, name="ws", align_bytes=64)
         nc.vector.memset(ws[:].rearrange("p g n -> p (g n)").bitcast(I32), 0)
-        w_by_p = w_words.rearrange("e a p b -> p (e a) b").bitcast(I32)
-        for i in range(2):
-            g = slice(i * E, (i + 1) * E)
-            nc.sync.dma_start(out=wt[:, g, :].bitcast(I32), in_=w_by_p[:, g, :])
         s_by_q = w_scales.rearrange("e a (q r) n -> q r (e a) n", r=4).bitcast(I32)
+        words = [load_words(0, "words0")]
         for q in range(4):
             nc.sync.dma_start(out=ws[32 * q : 32 * q + 4, :, :].bitcast(I32), in_=s_by_q[q])
         gt = keep.tile([P, E * C], F32, name="gt", align_bytes=64)
         nc.sync.dma_start(out=gt[:], in_=gate[0:P, :])
 
-        codes, scales = [], []
-        for a in range(PASSES):
-            c = keep.tile([P, T], U32, name=f"codes{a}", align_bytes=64)
-            s = keep.tile([P, T], U8, name=f"scales{a}", align_bytes=64)
-            nc.gpsimd.memset(s[:], 0)
-            codes.append(c)
-            scales.append(s)
+        codes = [keep.tile([P, T], U32, name=f"codes{a}", tag=f"codes{a}", align_bytes=64) for a in range(PASSES)]
+        planes = keep.tile([P, T], U8, name="planes", align_bytes=64)
+        nc.gpsimd.memset(planes[:], 0)
+        moved = keep.tile([P, E * C], U8, name="moved", align_bytes=64)
+        nc.gpsimd.memset(moved[:], 0)
 
         for a in range(PASSES):
             for t0, n, n_scalar in CHUNKS[a]:
@@ -78,53 +79,53 @@ def tile_moe_pln_lin_none_kernel(tc, xT, w_words, w_scales, gate, offs, out):
                 cols = slice(t0, t0 + n)
                 nc.vector.quantize_mx(
                     out=codes[a][:, cols].bitcast(FP8X4),
-                    scales=scales[a][:, cols],
+                    scales=planes[4 * a : P, cols],
                     in_=g[:].rearrange("p w j -> p (w j)"),
                 )
 
-        picked, picked_s = [], []
-        for a in range(PASSES):
-            c = keep.tile([P, E * C], U32, name=f"picked{a}", align_bytes=64)
-            s = keep.tile([P, E * C], U8, name=f"picked_s{a}", align_bytes=64)
-            picked.append(c)
-            picked_s.append(s)
-            for h in range(E * C // H):
-                cols = slice(h * H, (h + 1) * H)
-                idx = lists[:, h * H // 16 : (h + 1) * H // 16]
-                nc.vector.tensor_copy(c[:, cols], codes[a][:].indirect(idx))
-                nc.vector.tensor_copy(s[:, cols], scales[a][:].indirect(idx))
+        picked = [keep.tile([P, E * C], U32, name=f"picked{a}", align_bytes=64) for a in range(PASSES)]
+        picked_s = keep.tile([P, E * C], U8, name="picked_s", align_bytes=64)
 
-        banks = {}
+        def gather(table, picks, h):
+            idx = lists[:, h * H // 16 : (h + 1) * H // 16]
+            nc.vector.tensor_copy(picks[:, h * H : (h + 1) * H], table[:].indirect(idx))
+
+        gather(codes[0], picked[0], 0)
+        gather(codes[0], picked[0], 1)
         for h in range(2):
+            gather(planes, picked_s, h)
+            for r in range(4):
+                cols = slice(h * H, (h + 1) * H)
+                nc.sync.dma_start(out=moved[r:P:32, cols].bitcast(I32), in_=picked_s[4 + r : P : 32, cols].bitcast(I32))
+        for h in range(2):
+            gather(codes[1], picked[1], h)
+        planes_of = [picked_s, moved]
+        words.append(load_words(1, "codes1"))
+
+        back = [keep.tile([P, T], F32, name=f"back{m}", align_bytes=64) for m in range(2)]
+        pieces = ((0, 256), (256, 256), (512, 512))
+        sums = {}
+        for s0, n in pieces:
             for m in range(2):
-                bank = psum.tile([P, H], F32, name=f"bank{m}{h}")
-                banks[m, h] = bank
-                for i in range(H // C):
-                    e = h * (H // C) + i
+                bank = psum.tile([P, n], F32, name=f"bank{m}_{s0}")
+                for i in range(n // C):
+                    e = s0 // C + i
                     for a in range(PASSES):
                         nc.tensor.matmul_mx(
                             out=bank[:, i * C : (i + 1) * C],
-                            lhsT=wt[:, e * PASSES + a, m * 256 : (m + 1) * 256].bitcast(FP4X4),
+                            lhsT=words[e // 4][:, e % 4 * PASSES + a, m * 256 : (m + 1) * 256].bitcast(FP4X4),
                             lhsT_scale=ws[:, e * PASSES + a, m * 128 : (m + 1) * 128],
                             rhs=picked[a][:, e * C : (e + 1) * C].bitcast(FP8X4),
-                            rhs_scale=picked_s[a][:, e * C : (e + 1) * C],
+                            rhs_scale=planes_of[a][:, e * C : (e + 1) * C],
                             start=(a == 0),
                             stop=(a == PASSES - 1),
                         )
-
-        gated = {}
-        for h in range(2):
+                y = keep.tile([P, n], F32, name=f"sums{m}_{s0}", align_bytes=64)
+                nc.scalar.activation(y[:], bank[:], COPY)
+                sums[m, s0] = y
+        for s0, n in pieces:
             for m in range(2):
-                plain = keep.tile([P, H], F32, name=f"plain{m}{h}", align_bytes=64)
-                nc.scalar.activation(plain[:], banks[m, h][:], COPY)
-                gated[m, h] = plain
-        back = []
-        for m in range(2):
-            b = keep.tile([P, T], F32, name=f"back{m}", align_bytes=64)
-            back.append(b)
-        for h in range(2):
-            for m in range(2):
-                idx = lists[:, h * H // 16 : (h + 1) * H // 16]
-                nc.vector.tensor_tensor(back[m][:].indirect(idx), gated[m, h][:], gt[:, h * H : (h + 1) * H], MULT)
+                idx = lists[:, s0 // 16 : (s0 + n) // 16]
+                nc.vector.tensor_tensor(back[m][:].indirect(idx), sums[m, s0][:], gt[:, s0 : s0 + n], MULT)
         for m in range(2):
             nc.sync.dma_start(out=out[m * P : (m + 1) * P, :], in_=back[m][:])

from contextlib import ExitStack

import concourse.mybir as mybir

K, T, E, C, N = 1024, 1024, 8, 128, 256
FLOPS = 2 * K * E * C * N
BYTES = 4 * K * T + E * K * N // 2 + E * K * N // 32 + 4 * E * C + 2 * 128 * (E * C // 16) + 4 * N * T

F32 = mybir.dt.float32
BF16 = mybir.dt.bfloat16
U32 = mybir.dt.uint32
I32 = mybir.dt.int32
U16 = mybir.dt.uint16
U8 = mybir.dt.uint8
FP8X4 = mybir.dt.float8_e4m3fn_x4
FP4X4 = mybir.dt.float4_e2m1fn_x4
COPY = mybir.ActivationFunctionType.Copy
MULT = mybir.AluOpType.mult

P = 128
PASSES = K // 512
H = 512
CHUNKS = (
    ((0, 512, 256), (512, 256, 128), (768, 256, 88)),
    ((0, 256, 256), (256, 256, 256), (512, 256, 256), (768, 256, 160)),
)


def tile_moe_pln_lin_none_kernel(tc, xT, w_words, w_scales, gate, offs, out):
    nc = tc.nc
    with ExitStack() as ctx:
        keep = ctx.enter_context(tc.tile_pool(name="keep", bufs=1))
        psum = ctx.enter_context(tc.psum_pool(name="psum", bufs=1))

        lists = keep.tile([P, E * C // 16], U16, name="lists")
        raw = {}
        for a in range(PASSES):
            for t0, n, n_scalar in CHUNKS[a]:
                r = keep.tile([P, 4, n], F32, name=f"raw{a}_{t0}", align_bytes=64)
                nc.sync.dma_start(
                    out=r[:],
                    in_=xT[a * 512 : (a + 1) * 512, t0 : t0 + n].rearrange("(p j) w -> p j w", j=4),
                )
                raw[a, t0] = r
            if a == 0:
                nc.sync.dma_start(lists[:], offs)

        w_by_p = w_words.rearrange("e a p b -> p (e a) b").bitcast(I32)

        def load_words(h, tag):
            t = keep.tile([P, E, 2 * N], U8, name=f"words{h}", tag=tag, align_bytes=64)
            nc.sync.dma_start(out=t[:].bitcast(I32), in_=w_by_p[:, h * E : (h + 1) * E, :])
            return t

        ws = keep.tile([P, E * PASSES, N], U8, name="ws", align_bytes=64)
        nc.vector.memset(ws[:].rearrange("p g n -> p (g n)").bitcast(I32), 0)
        s_by_q = w_scales.rearrange("e a (q r) n -> q r (e a) n", r=4).bitcast(I32)
        words = [load_words(0, "words0")]
        for q in range(4):
            nc.sync.dma_start(out=ws[32 * q : 32 * q + 4, :, :].bitcast(I32), in_=s_by_q[q])
        gt = keep.tile([P, E * C], F32, name="gt", align_bytes=64)
        nc.sync.dma_start(out=gt[:], in_=gate[0:P, :])

        codes = [keep.tile([P, T], U32, name=f"codes{a}", tag=f"codes{a}", align_bytes=64) for a in range(PASSES)]
        planes = keep.tile([P, T], U8, name="planes", align_bytes=64)
        nc.gpsimd.memset(planes[:], 0)
        moved = keep.tile([P, E * C], U8, name="moved", align_bytes=64)
        nc.gpsimd.memset(moved[:], 0)

        for a in range(PASSES):
            for t0, n, n_scalar in CHUNKS[a]:
                g = keep.tile([P, n, 4], BF16, name=f"grouped{a}_{t0}", align_bytes=64)
                src = raw[a, t0][:].rearrange("p j (c i) -> p c j i", i=4)
                dst = g[:].rearrange("p (c i) j -> p c j i", i=4)
                cut = n_scalar // 4
                nc.scalar.activation(dst[:, 0:cut], src[:, 0:cut], COPY)
                if n_scalar < n:
                    nc.vector.tensor_copy(dst[:, cut : n // 4], src[:, cut : n // 4])
                cols = slice(t0, t0 + n)
                nc.vector.quantize_mx(
                    out=codes[a][:, cols].bitcast(FP8X4),
                    scales=planes[4 * a : P, cols],
                    in_=g[:].rearrange("p w j -> p (w j)"),
                )

        picked = [keep.tile([P, E * C], U32, name=f"picked{a}", align_bytes=64) for a in range(PASSES)]
        picked_s = keep.tile([P, E * C], U8, name="picked_s", align_bytes=64)

        def gather(table, picks, h):
            idx = lists[:, h * H // 16 : (h + 1) * H // 16]
            nc.vector.tensor_copy(picks[:, h * H : (h + 1) * H], table[:].indirect(idx))

        gather(codes[0], picked[0], 0)
        gather(codes[0], picked[0], 1)
        for h in range(2):
            gather(planes, picked_s, h)
            for r in range(4):
                cols = slice(h * H, (h + 1) * H)
                nc.sync.dma_start(out=moved[r:P:32, cols].bitcast(I32), in_=picked_s[4 + r : P : 32, cols].bitcast(I32))
        for h in range(2):
            gather(codes[1], picked[1], h)
        planes_of = [picked_s, moved]
        words.append(load_words(1, "codes1"))

        back = [keep.tile([P, T], F32, name=f"back{m}", align_bytes=64) for m in range(2)]
        pieces = ((0, 256), (256, 256), (512, 512))
        sums = {}
        for s0, n in pieces:
            for m in range(2):
                bank = psum.tile([P, n], F32, name=f"bank{m}_{s0}")
                for i in range(n // C):
                    e = s0 // C + i
                    for a in range(PASSES):
                        nc.tensor.matmul_mx(
                            out=bank[:, i * C : (i + 1) * C],
                            lhsT=words[e // 4][:, e % 4 * PASSES + a, m * 256 : (m + 1) * 256].bitcast(FP4X4),
                            lhsT_scale=ws[:, e * PASSES + a, m * 128 : (m + 1) * 128],
                            rhs=picked[a][:, e * C : (e + 1) * C].bitcast(FP8X4),
                            rhs_scale=planes_of[a][:, e * C : (e + 1) * C],
                            start=(a == 0),
                            stop=(a == PASSES - 1),
                        )
                y = keep.tile([P, n], F32, name=f"sums{m}_{s0}", align_bytes=64)
                nc.scalar.activation(y[:], bank[:], COPY)
                sums[m, s0] = y
        for s0, n in pieces:
            for m in range(2):
                idx = lists[:, s0 // 16 : (s0 + n) // 16]
                nc.vector.tensor_tensor(back[m][:].indirect(idx), sums[m, s0][:], gt[:, s0 : s0 + n], MULT)
        for m in range(2):
            nc.sync.dma_start(out=out[m * P : (m + 1) * P, :], in_=back[m][:])
